import numpy as np
import ml_dtypes

BF16 = ml_dtypes.bfloat16


def bf(x):
    return np.asarray(x, np.float32).astype(BF16)


def f32(x):
    return np.asarray(x, np.float32)


def f64(x):
    return np.asarray(x).astype(np.float64)


def striped(idx):
    return np.concatenate([l.reshape(-1, 16).T for l in idx])


def rows(idx, k):
    return np.tile(np.repeat(idx, 16, axis=0), (k // (16 * 8), 1))


def look(tab, idx):
    return np.take_along_axis(f64(tab), rows(idx, len(tab)), axis=1)


K, S, V, N, M = 256, 2048, 2048, 2048, 512


def silu(v):
    return v / (1.0 + np.exp(-v))


def setup_inputs():
    return {"tab": f32(np.random.standard_normal((2, K, S))), "y": f32(np.random.standard_normal((K, V))), "w": bf(np.random.standard_normal((K, M)) / np.sqrt(K)), "b": f32(0.5 * np.random.standard_normal((M, 1))), "offs": striped(np.stack([np.random.permutation(S)[:N] for _ in range(8)]))}


def reference(tab, y, w, b, offs):
    idx = np.stack([g.T.reshape(-1) for g in np.split(offs, 8)])
    x = (look(tab[0], idx) + f64(y)) * (silu(look(tab[1], idx)))
    return np.maximum(f64(w).T @ x + f64(b), 0.0)

@@ -1,0 +1,67 @@
+import concourse.mybir as mybir
+
+F32, BF16, U16 = mybir.dt.float32, mybir.dt.bfloat16, mybir.dt.uint16
+ADD, MULT, MAX = mybir.AluOpType.add, mybir.AluOpType.mult, mybir.AluOpType.max
+SILU, RELU = mybir.ActivationFunctionType.Silu, mybir.ActivationFunctionType.Relu
+
+P = 128
+GROUP = 16
+PIECE = 512
+K, N, M = 256, 2048, 512
+FLOPS = 2 * K * M * N
+
+
+def tile_lookup_vg_addsilu_relu_kernel(tc, tab, y, w, b, offs, out):
+    nc = tc.nc
+    places = tab.shape[2]
+    blocks, pieces, m_blocks = K // P, N // PIECE, M // P
+    half = N // 2
+    out_rows = out.rearrange("(p c) n -> p c n", c=m_blocks)
+
+    with (
+        tc.tile_pool(name="held", bufs=1) as held,
+        tc.tile_pool(name="work", bufs=4) as work,
+        tc.psum_pool(name="psum", bufs=2) as psum,
+    ):
+        offsets = held.tile([P, N // GROUP], U16, name="offsets")
+        nc.sync.dma_start(offsets[:], offs)
+
+        gates, values, streams = [], [], []
+        for r in range(blocks):
+            rows = slice(r * P, (r + 1) * P)
+            gates.append(held.tile([P, places], F32, name=f"gate{r}"))
+            values.append(held.tile([P, places], F32, name=f"value{r}"))
+            streams.append(held.tile([P, N], F32, name=f"stream{r}"))
+            nc.sync.dma_start(gates[r][:], tab[1, rows, :])
+            nc.sync.dma_start(values[r][:], tab[0, rows, :])
+            nc.sync.dma_start(streams[r][:, :half], y[rows, :half])
+            if r == blocks - 1:
+                weights = held.tile([P, blocks, M], BF16, name="weights")
+                nc.sync.dma_start(weights[:], w.rearrange("(r p) m -> p r m", p=P))
+                bias = held.tile([P, m_blocks], F32, name="bias")
+                nc.sync.dma_start(bias[:], b.rearrange("(p c) o -> p (c o)", c=m_blocks))
+            nc.sync.dma_start(streams[r][:, half:], y[rows, half:])
+
+        x = [held.tile([P, N], BF16, name=f"x{r}") for r in range(blocks)]
+        for r in range(blocks):
+            for j in range(pieces):
+                cols = slice(j * PIECE, (j + 1) * PIECE)
+                entries = offsets[:, j * PIECE // GROUP : (j + 1) * PIECE // GROUP]
+                opened = work.tile([P, PIECE], F32, name="opened")
+                summed = work.tile([P, PIECE], F32, name="summed")
+                nc.scalar.activation(opened[:], gates[r][:].indirect(entries), SILU)
+                nc.vector.tensor_tensor(summed[:], values[r][:].indirect(entries), streams[r][:, cols], ADD)
+                nc.vector.tensor_tensor(x[r][:, cols], summed[:], opened[:], MULT)
+                if r < blocks - 1:
+                    continue
+                result = work.tile([P, m_blocks, PIECE], F32, name="result")
+                for c in range(m_blocks):
+                    acc = psum.tile([P, PIECE], F32, name=f"acc{c}")
+                    for k in range(blocks):
+                        nc.tensor.matmul(acc[:], weights[:, k, c::m_blocks], x[k][:, cols],
+                                         start=(k == 0), stop=(k == blocks - 1))
+                    if j == pieces - 1 and c % 2 == 1:
+                        nc.vector.tensor_scalar(result[:, c, :], acc[:], bias[:, c : c + 1], 0.0, ADD, MAX)
+                    else:
+                        nc.scalar.activation(result[:, c, :], acc[:], RELU, bias=bias[:, c : c + 1])
+                    nc.sync.dma_start(out_rows[:, c, cols], result[:, c, :])

@@ -7,6 +7,7 @@ SILU, RELU = mybir.ActivationFunctionType.Silu, mybir.ActivationFunctionType.Rel
 P = 128
 GROUP = 16
 PIECE = 512
+LEAD = 3
 K, N, M = 256, 2048, 512
 FLOPS = 2 * K * M * N
 
@@ -15,7 +16,8 @@ def tile_lookup_vg_addsilu_relu_kernel(tc, tab, y, w, b, offs, out):
     nc = tc.nc
     places = tab.shape[2]
     blocks, pieces, m_blocks = K // P, N // PIECE, M // P
-    half = N // 2
+    lead = LEAD * PIECE
+    rows = [slice(r * P, (r + 1) * P) for r in range(blocks)]
     out_rows = out.rearrange("(p c) n -> p c n", c=m_blocks)
 
     with (
@@ -24,44 +26,48 @@ def tile_lookup_vg_addsilu_relu_kernel(tc, tab, y, w, b, offs, out):
         tc.psum_pool(name="psum", bufs=2) as psum,
     ):
         offsets = held.tile([P, N // GROUP], U16, name="offsets")
-        nc.sync.dma_start(offsets[:], offs)
-
-        gates, values, streams = [], [], []
-        for r in range(blocks):
-            rows = slice(r * P, (r + 1) * P)
-            gates.append(held.tile([P, places], F32, name=f"gate{r}"))
-            values.append(held.tile([P, places], F32, name=f"value{r}"))
-            streams.append(held.tile([P, N], F32, name=f"stream{r}"))
-            nc.sync.dma_start(gates[r][:], tab[1, rows, :])
-            nc.sync.dma_start(values[r][:], tab[0, rows, :])
-            nc.sync.dma_start(streams[r][:, :half], y[rows, :half])
-            if r == blocks - 1:
-                weights = held.tile([P, blocks, M], BF16, name="weights")
-                nc.sync.dma_start(weights[:], w.rearrange("(r p) m -> p r m", p=P))
-                bias = held.tile([P, m_blocks], F32, name="bias")
-                nc.sync.dma_start(bias[:], b.rearrange("(p c) o -> p (c o)", c=m_blocks))
-            nc.sync.dma_start(streams[r][:, half:], y[rows, half:])
-
+        gates = [held.tile([P, places], F32, name=f"gate{r}") for r in range(blocks)]
+        values = [held.tile([P, places], F32, name=f"value{r}") for r in range(blocks)]
+        streams = [held.tile([P, N], F32, name=f"stream{r}") for r in range(blocks)]
+        opened = [held.tile([P, N], F32, name=f"opened{r}") for r in range(blocks)]
         x = [held.tile([P, N], BF16, name=f"x{r}") for r in range(blocks)]
+        weights = [held.tile([P, M], BF16, name=f"weights{r}") for r in range(blocks)]
+        bias = held.tile([P, m_blocks], F32, name="bias")
+
+        nc.sync.dma_start(offsets[:], offs)
+        nc.sync.dma_start(bias[:], b.rearrange("(p c) o -> p (c o)", c=m_blocks))
+        for r in range(blocks):
+            nc.sync.dma_start(gates[r][:], tab[1, rows[r], :])
+            nc.sync.dma_start(streams[r][:, :PIECE], y[rows[r], :PIECE])
+            nc.sync.dma_start(values[r][:], tab[0, rows[r], :])
+            nc.sync.dma_start(weights[r][:], w[rows[r], :])
+            nc.sync.dma_start(streams[r][:, PIECE:lead], y[rows[r], PIECE:lead])
+        for r in range(blocks):
+            nc.sync.dma_start(streams[r][:, lead:], y[rows[r], lead:])
+
+        cols = [slice(j * PIECE, (j + 1) * PIECE) for j in range(pieces)]
+        entries = [offsets[:, j * PIECE // GROUP : (j + 1) * PIECE // GROUP] for j in range(pieces)]
+
         for r in range(blocks):
             for j in range(pieces):
-                cols = slice(j * PIECE, (j + 1) * PIECE)
-                entries = offsets[:, j * PIECE // GROUP : (j + 1) * PIECE // GROUP]
-                opened = work.tile([P, PIECE], F32, name="opened")
-                summed = work.tile([P, PIECE], F32, name="summed")
-                nc.scalar.activation(opened[:], gates[r][:].indirect(entries), SILU)
-                nc.vector.tensor_tensor(summed[:], values[r][:].indirect(entries), streams[r][:, cols], ADD)
-                nc.vector.tensor_tensor(x[r][:, cols], summed[:], opened[:], MULT)
-                if r < blocks - 1:
-                    continue
-                result = work.tile([P, m_blocks, PIECE], F32, name="result")
-                for c in range(m_blocks):
-                    acc = psum.tile([P, PIECE], F32, name=f"acc{c}")
-                    for k in range(blocks):
-                        nc.tensor.matmul(acc[:], weights[:, k, c::m_blocks], x[k][:, cols],
-                                         start=(k == 0), stop=(k == blocks - 1))
-                    if j == pieces - 1 and c % 2 == 1:
-                        nc.vector.tensor_scalar(result[:, c, :], acc[:], bias[:, c : c + 1], 0.0, ADD, MAX)
-                    else:
-                        nc.scalar.activation(result[:, c, :], acc[:], RELU, bias=bias[:, c : c + 1])
-                    nc.sync.dma_start(out_rows[:, c, cols], result[:, c, :])
+                nc.scalar.activation(opened[r][:, cols[j]], gates[r][:].indirect(entries[j]), SILU)
+
+        for span in (range(LEAD), range(LEAD, pieces)):
+            for r in range(blocks):
+                for j in span:
+                    summed = work.tile([P, PIECE], F32, name="summed")
+                    nc.vector.tensor_tensor(summed[:], values[r][:].indirect(entries[j]), streams[r][:, cols[j]], ADD)
+                    nc.vector.tensor_tensor(x[r][:, cols[j]], summed[:], opened[r][:, cols[j]], MULT)
+
+        for j in range(pieces):
+            result = work.tile([P, m_blocks, PIECE], F32, name="result")
+            for c in range(m_blocks):
+                acc = psum.tile([P, PIECE], F32, name=f"acc{c}")
+                for r in range(blocks):
+                    nc.tensor.matmul(acc[:], weights[r][:, c::m_blocks], x[r][:, cols[j]],
+                                     start=(r == 0), stop=(r == blocks - 1))
+                if j == pieces - 1 and c < m_blocks - 1:
+                    nc.vector.tensor_scalar(result[:, c, :], acc[:], bias[:, c : c + 1], 0.0, ADD, MAX)
+                else:
+                    nc.scalar.activation(result[:, c, :], acc[:], RELU, bias=bias[:, c : c + 1])
+                nc.sync.dma_start(out_rows[:, c, cols[j]], result[:, c, :])

@@ -31,17 +31,18 @@ def tile_lookup_vg_addsilu_relu_kernel(tc, tab, y, w, b, offs, out):
         streams = [held.tile([P, N], F32, name=f"stream{r}") for r in range(blocks)]
         opened = [held.tile([P, N], F32, name=f"opened{r}") for r in range(blocks)]
         x = [held.tile([P, N], BF16, name=f"x{r}") for r in range(blocks)]
-        weights = [held.tile([P, M], BF16, name=f"weights{r}") for r in range(blocks)]
+        weights = held.tile([P, blocks, M], BF16, name="weights")
         bias = held.tile([P, m_blocks], F32, name="bias")
 
         nc.sync.dma_start(offsets[:], offs)
-        nc.sync.dma_start(bias[:], b.rearrange("(p c) o -> p (c o)", c=m_blocks))
         for r in range(blocks):
             nc.sync.dma_start(gates[r][:], tab[1, rows[r], :])
             nc.sync.dma_start(streams[r][:, :PIECE], y[rows[r], :PIECE])
             nc.sync.dma_start(values[r][:], tab[0, rows[r], :])
-            nc.sync.dma_start(weights[r][:], w[rows[r], :])
+            if r == blocks - 1:
+                nc.sync.dma_start(weights[:], w.rearrange("(r p) m -> p r m", p=P))
             nc.sync.dma_start(streams[r][:, PIECE:lead], y[rows[r], PIECE:lead])
+        nc.sync.dma_start(bias[:], b.rearrange("(p c) o -> p (c o)", c=m_blocks))
         for r in range(blocks):
             nc.sync.dma_start(streams[r][:, lead:], y[rows[r], lead:])
 
@@ -64,7 +65,7 @@ def tile_lookup_vg_addsilu_relu_kernel(tc, tab, y, w, b, offs, out):
             for c in range(m_blocks):
                 acc = psum.tile([P, PIECE], F32, name=f"acc{c}")
                 for r in range(blocks):
-                    nc.tensor.matmul(acc[:], weights[r][:, c::m_blocks], x[r][:, cols[j]],
+                    nc.tensor.matmul(acc[:], weights[:, r, c::m_blocks], x[r][:, cols[j]],
                                      start=(r == 0), stop=(r == blocks - 1))
                 if j == pieces - 1 and c < m_blocks - 1:
                     nc.vector.tensor_scalar(result[:, c, :], acc[:], bias[:, c : c + 1], 0.0, ADD, MAX)

import concourse.mybir as mybir

F32, BF16, U16 = mybir.dt.float32, mybir.dt.bfloat16, mybir.dt.uint16
ADD, MULT, MAX = mybir.AluOpType.add, mybir.AluOpType.mult, mybir.AluOpType.max
SILU, RELU = mybir.ActivationFunctionType.Silu, mybir.ActivationFunctionType.Relu

P = 128
GROUP = 16
PIECE = 512
LEAD = 3
K, N, M = 256, 2048, 512
FLOPS = 2 * K * M * N


def tile_lookup_vg_addsilu_relu_kernel(tc, tab, y, w, b, offs, out):
    nc = tc.nc
    places = tab.shape[2]
    blocks, pieces, m_blocks = K // P, N // PIECE, M // P
    lead = LEAD * PIECE
    rows = [slice(r * P, (r + 1) * P) for r in range(blocks)]
    out_rows = out.rearrange("(p c) n -> p c n", c=m_blocks)

    with (
        tc.tile_pool(name="held", bufs=1) as held,
        tc.tile_pool(name="work", bufs=4) as work,
        tc.psum_pool(name="psum", bufs=2) as psum,
    ):
        offsets = held.tile([P, N // GROUP], U16, name="offsets")
        gates = [held.tile([P, places], F32, name=f"gate{r}") for r in range(blocks)]
        values = [held.tile([P, places], F32, name=f"value{r}") for r in range(blocks)]
        streams = [held.tile([P, N], F32, name=f"stream{r}") for r in range(blocks)]
        opened = [held.tile([P, N], F32, name=f"opened{r}") for r in range(blocks)]
        x = [held.tile([P, N], BF16, name=f"x{r}") for r in range(blocks)]
        weights = held.tile([P, blocks, M], BF16, name="weights")
        bias = held.tile([P, m_blocks], F32, name="bias")

        nc.sync.dma_start(offsets[:], offs)
        for r in range(blocks):
            nc.sync.dma_start(gates[r][:], tab[1, rows[r], :])
            nc.sync.dma_start(streams[r][:, :PIECE], y[rows[r], :PIECE])
            nc.sync.dma_start(values[r][:], tab[0, rows[r], :])
            if r == blocks - 1:
                nc.sync.dma_start(weights[:], w.rearrange("(r p) m -> p r m", p=P))
            nc.sync.dma_start(streams[r][:, PIECE:lead], y[rows[r], PIECE:lead])
        nc.sync.dma_start(bias[:], b.rearrange("(p c) o -> p (c o)", c=m_blocks))
        for r in range(blocks):
            nc.sync.dma_start(streams[r][:, lead:], y[rows[r], lead:])

        cols = [slice(j * PIECE, (j + 1) * PIECE) for j in range(pieces)]
        entries = [offsets[:, j * PIECE // GROUP : (j + 1) * PIECE // GROUP] for j in range(pieces)]

        for r in range(blocks):
            for j in range(pieces):
                nc.scalar.activation(opened[r][:, cols[j]], gates[r][:].indirect(entries[j]), SILU)

        for span in (range(LEAD), range(LEAD, pieces)):
            for r in range(blocks):
                for j in span:
                    summed = work.tile([P, PIECE], F32, name="summed")
                    nc.vector.tensor_tensor(summed[:], values[r][:].indirect(entries[j]), streams[r][:, cols[j]], ADD)
                    nc.vector.tensor_tensor(x[r][:, cols[j]], summed[:], opened[r][:, cols[j]], MULT)

        for j in range(pieces):
            result = work.tile([P, m_blocks, PIECE], F32, name="result")
            for c in range(m_blocks):
                acc = psum.tile([P, PIECE], F32, name=f"acc{c}")
                for r in range(blocks):
                    nc.tensor.matmul(acc[:], weights[:, r, c::m_blocks], x[r][:, cols[j]],
                                     start=(r == 0), stop=(r == blocks - 1))
                if j == pieces - 1 and c < m_blocks - 1:
                    nc.vector.tensor_scalar(result[:, c, :], acc[:], bias[:, c : c + 1], 0.0, ADD, MAX)
                else:
                    nc.scalar.activation(result[:, c, :], acc[:], RELU, bias=bias[:, c : c + 1])
                nc.sync.dma_start(out_rows[:, c, cols[j]], result[:, c, :])
